import numpy as np
import ml_dtypes


def mxq(x, axis, fmt="e4m3"):
    dtype, down = {"e4m3": (ml_dtypes.float8_e4m3fn, 7), "e5m2": (ml_dtypes.float8_e5m2, 14)}[fmt]
    v = np.moveaxis(np.asarray(x, np.float32).astype(ml_dtypes.bfloat16).astype(np.float64), axis, -1)
    blocks = v.reshape(v.shape[:-1] + (-1, 32))
    amax = np.abs(blocks).max(-1, keepdims=True)
    byte = np.maximum(np.where(amax > 0, np.frexp(amax)[1] - 1 + 127, 0) - down, 1)
    scale = np.exp2(byte - 127.0)
    codes = (blocks / scale).astype(np.float32).astype(dtype).astype(np.float64)
    return np.moveaxis((codes * scale).reshape(v.shape), -1, axis)


WIDE = False


def mx_kscale(k):
    if not WIDE:
        return np.ones(k)
    levels = np.array([10, -10, 5, -5, 0])
    if k % 512:
        return np.exp2(np.random.permutation(np.resize(levels, k // 32))).repeat(32)
    a = np.empty((k // 512, 16))
    for p in range(k // 512):
        a[p, :8] = np.random.permutation(np.resize(levels, 8))
        for g in range(8):
            far = levels[np.abs(levels - a[p, g]) >= 10]
            a[p, g + 8] = far[np.random.randint(len(far))]
    return np.exp2(a.ravel()).repeat(32)


BF16 = ml_dtypes.bfloat16


def bf(x):
    return np.asarray(x, np.float32).astype(BF16)


def f64(x):
    return np.asarray(x).astype(np.float64)


V, P, D, H = 8, 1024, 1024, 512


def softmax0(a):
    z = np.exp(a - a.max(axis=0, keepdims=True))
    return z / z.sum(axis=0, keepdims=True)


def view_statistics(f, om):
    w = om[:, :, None]
    mu = np.sum(w * f, axis=0)
    diff = f - mu[None, :, :]
    var = np.sum(w * (diff * diff), axis=0)
    return mu, var


def elu_unit(e):
    return np.maximum(e, 0.0) + np.exp(np.minimum(e, 0.0)) - 1.0


def draw0():
    s, t, u = mx_kscale(D), mx_kscale(D), mx_kscale(D)
    r = 1.0 / np.sqrt(D)
    return {
        "f": bf(np.random.standard_normal((V, P, D)) * s),
        "lw": bf(np.random.standard_normal((V, P))),
        "gm": bf((1.0 + 0.1 * np.random.standard_normal(D)) * t / s),
        "gv": bf(np.random.standard_normal(D) * u / (s * s)),
        "wf": bf(np.random.standard_normal((D, H)) * r / s[:, None]),
        "wm": bf(np.random.standard_normal((D, H)) * 1.5 * r / t[:, None]),
        "wv": bf(np.random.standard_normal((D, H)) * r / u[:, None]),
    }


def core(f, lw, gm, gv, wf, wm, wv):
    x = f64(f)
    om = softmax0(f64(lw))
    mu, var = view_statistics(x, om)
    a = mu * f64(gm)[None, :]
    b = var * f64(gv)[None, :]
    c = (mxq(a, 1, "e4m3") @ mxq(f64(wm), 0, "e4m3")) + (mxq(b, 1, "e4m3") @ mxq(f64(wv), 0, "e4m3"))
    e = (mxq(x, 2, "e4m3") @ mxq(f64(wf), 0, "e4m3")) + c[None, :, :]
    return elu_unit(e)


def e4m3fn_bytes(y):
    return np.clip(np.asarray(y, np.float64), -448.0, 448.0).astype(np.float32).astype(ml_dtypes.float8_e4m3fn).view(np.uint8)


def e4m3fn_values(b):
    return np.asarray(b, np.uint8).view(ml_dtypes.float8_e4m3fn).astype(np.float64)


def setup_inputs():
    d = draw0()
    x0 = np.asarray(d['wv']).astype(np.float64)
    s = (np.max(np.abs(x0), axis=(1,), keepdims=True) / 448.0).astype(np.float32)
    out = {}
    for k, v in d.items():
        if k == 'wv':
            out['wv_bytes'] = e4m3fn_bytes(x0 / s.astype(np.float64))
            out['wv_scale'] = s
        else:
            out[k] = v
    return out


def reference(f, lw, gm, gv, wf, wm, wv_bytes, wv_scale):
    return core(f, lw, gm, gv, wf, wm, e4m3fn_values(wv_bytes) * wv_scale.astype(np.float64))

@@ -1,0 +1,370 @@
+from contextlib import ExitStack
+
+import concourse.mybir as mybir
+from concourse.masks import make_identity
+
+V, P, D, H = 8, 1024, 1024, 512
+FLOPS = 2 * V * P * D * H + 2 * (2 * P * D * H)
+
+F32 = mybir.dt.float32
+BF16 = mybir.dt.bfloat16
+U32 = mybir.dt.uint32
+U8 = mybir.dt.uint8
+FP8 = mybir.dt.float8_e4m3fn
+FP8X4 = mybir.dt.float8_e4m3fn_x4
+ALU = mybir.AluOpType
+ACT = mybir.ActivationFunctionType
+AX = mybir.AxisListType
+
+PT = 128
+NP = P // PT
+G = D // 512
+T = 4
+PAIRS = V // 2
+A_STEPS = NP * PAIRS
+LAG_BANK = 3
+LAG_C = 8
+WITH_C = (27, 29, 31)
+BY_RELU = tuple(n for n in range(A_STEPS) if n >= 24 or n % 5 in (1, 3))
+LAG_E = 9
+
+
+def tile_ibrnetviewstatisticsmixer_t_kernel(tc, f, lw, gm, gv, wf, wm, wv_bytes, wv_scale, out):
+    nc = tc.nc
+    with ExitStack() as ctx:
+        keep = ctx.enter_context(tc.tile_pool(name="keep", bufs=1))
+        fp = ctx.enter_context(tc.tile_pool(name="fp", bufs=4))
+        gp = ctx.enter_context(tc.tile_pool(name="gp", bufs=6))
+        qp = ctx.enter_context(tc.tile_pool(name="qp", bufs=8))
+        xp = ctx.enter_context(tc.tile_pool(name="xp", bufs=2))
+        cp = ctx.enter_context(tc.tile_pool(name="cp", bufs=10))
+        ep = ctx.enter_context(tc.tile_pool(name="ep", bufs=3))
+        sp = ctx.enter_context(tc.tile_pool(name="sp", bufs=2))
+        ps_x = ctx.enter_context(tc.psum_pool(name="ps_x", bufs=3))
+        ps_a = ctx.enter_context(tc.psum_pool(name="ps_a", bufs=2))
+        ps_m = ctx.enter_context(tc.psum_pool(name="ps_m", bufs=3))
+
+        ident = keep.tile([128, 128], F32, name="ident")
+        make_identity(nc, ident[:])
+
+        def load_pair(s):
+            p0 = (s // PAIRS) * PT
+            v0 = 2 * (s % PAIRS)
+            t = fp.tile([128, 2, D], BF16, name="f_pair", align_bytes=64)
+            nc.sync.dma_start(out=t[:], in_=f[v0 : v0 + 2, p0 : p0 + PT, :].rearrange("v p d -> p v d"))
+            return t
+
+        f_pairs = {}
+
+        lw_rows = keep.tile([128, 128], BF16, name="lw_rows")
+        nc.vector.memset(lw_rows[64:128, :], 0.0)
+        nc.sync.dma_start(out=lw_rows[0:64, :], in_=lw.rearrange("v (t p) -> (v t) p", p=PT))
+        f_pairs[0] = load_pair(0)
+        gmv = keep.tile([128, G, T], BF16, name="gmv")
+        nc.sync.dma_start(out=gmv[:], in_=gm.rearrange("(g p t) -> p g t", p=128, t=T))
+        gvt = keep.tile([128, G, T], BF16, name="gvt")
+        nc.sync.dma_start(out=gvt[:], in_=gv.rearrange("(g p t) -> p g t", p=128, t=T))
+        wsc = keep.tile([128, G, T], F32, name="wsc")
+        nc.sync.dma_start(out=wsc[:], in_=wv_scale.rearrange("(g p t) o -> p g (t o)", p=128, t=T))
+
+        lw_f = keep.tile([128, 128], F32, name="lw_f")
+        nc.vector.tensor_copy(out=lw_f[:], in_=lw_rows[:])
+        lw_t = ps_x.tile([128, 2, 2, 128], F32, name="xt")
+        nc.tensor.transpose(lw_t[:, 0, 0, :], lw_f[:], ident[:])
+        z = keep.tile([128, V, NP], F32, name="z")
+        nc.vector.tensor_copy(out=z[:].rearrange("p v t -> p (v t)"), in_=lw_t[:, 0, 0, 0:64])
+        mx = keep.tile([128, NP], F32, name="mx")
+        nc.vector.reduce_max(mx[:], z[:].rearrange("p v t -> p t v"), axis=AX.X)
+        zs = keep.tile([128, V, NP], F32, name="zs")
+        nc.vector.tensor_tensor(out=zs[:], in0=z[:], in1=mx[:].unsqueeze(1).to_broadcast([128, V, NP]), op=ALU.subtract)
+        om = keep.tile([128, V, NP], F32, name="om")
+        rt = keep.tile([128, V, NP], F32, name="rt")
+        nc.scalar.activation(om[:], zs[:], ACT.Exp)
+        nc.scalar.activation(rt[:], zs[:], ACT.Exp, scale=0.5)
+        tot = keep.tile([128, NP], F32, name="tot")
+        nc.vector.reduce_sum(tot[:], om[:].rearrange("p v t -> p t v"), axis=AX.X)
+        inv = keep.tile([128, NP], F32, name="inv")
+        nc.vector.reciprocal(inv[:], tot[:])
+        y0 = keep.tile([128, NP], F32, name="y0")
+        nc.scalar.activation(y0[:], inv[:], ACT.Sqrt)
+        y1 = keep.tile([128, NP], F32, name="y1")
+        nc.vector.reciprocal(y1[:], y0[:])
+        nc.vector.tensor_tensor(out=y1[:], in0=y1[:], in1=inv[:], op=ALU.mult)
+        nc.vector.tensor_tensor(out=y1[:], in0=y1[:], in1=y0[:], op=ALU.add)
+        nc.vector.tensor_scalar(out=y1[:], in0=y1[:], scalar1=0.5, scalar2=None, op0=ALU.mult)
+        nc.vector.tensor_tensor(out=om[:], in0=om[:], in1=inv[:].unsqueeze(1).to_broadcast([128, V, NP]), op=ALU.mult)
+        nc.vector.tensor_tensor(out=rt[:], in0=rt[:], in1=y1[:].unsqueeze(1).to_broadcast([128, V, NP]), op=ALU.mult)
+
+        codes_w = {}
+        scales_w = {}
+        for nm in ("wf", "wm", "wv"):
+            codes_w[nm] = keep.tile([128, G, H], U32, name="codes_" + nm, align_bytes=64)
+            scales_w[nm] = keep.tile([128, G, H], U8, name="scales_" + nm, align_bytes=64)
+        wv8 = keep.tile([128, G, T * H], U8, name="wv8")
+
+        def load_weight(w, g):
+            raw = ep.tile([128, T, H], BF16, name="raw", tag="e", align_bytes=64)
+            nc.sync.dma_start(out=raw[:], in_=w.rearrange("(g p t) n -> g p t n", p=128, t=T)[g])
+            return raw
+
+        def widen_wv(g):
+            raw = ep.tile([128, T, H], BF16, name="raw", tag="e", align_bytes=64)
+            for t in range(T):
+                nc.vector.tensor_scalar(
+                    out=raw[:, t, :], in0=wv8[:, g, t * H : (t + 1) * H].bitcast(FP8), scalar1=wsc[:, g, t : t + 1], scalar2=None, op0=ALU.mult
+                )
+            return raw
+
+        def interleave(raw):
+            grp = ep.tile([128, H, T], BF16, name="grp", tag="m", align_bytes=64)
+            nc.vector.tensor_copy(
+                out=grp[:].rearrange("p (c i) t -> p c t i", i=4), in_=raw[:].rearrange("p t (c i) -> p c t i", i=4)
+            )
+            return grp
+
+        def quantize_weight(grp, nm, g):
+            nc.vector.quantize_mx(
+                out=codes_w[nm][:, g, :].bitcast(FP8X4), scales=scales_w[nm][:, g, :], in_=grp[:].rearrange("p n t -> p (n t)")
+            )
+
+        xs = {}
+        xg = {}
+        codes = {}
+        g_t = {}
+        q_t = {}
+        bank = {}
+        musq = {}
+        ab = {}
+        abc = {}
+        c_ps = {}
+        c_sb = {}
+        mm = {}
+        e_t = {}
+        m_t = {}
+        var_t = {}
+
+        def transposes(s):
+            words = f_pairs[s][:].rearrange("p v d -> p (v d)").bitcast(F32)
+            for v in range(2):
+                xt = ps_x.tile([128, 2, 2, 128], F32, name="xt")
+                for g in range(G):
+                    for u in range(2):
+                        w0 = 512 * v + 256 * g
+                        nc.tensor.transpose(xt[:, g, u, :], words[:, w0 + u : w0 + 256 : 2], ident[:])
+                xs[s, v] = xt
+
+        def evacuate(s):
+            t = xp.tile([128, 2, G, 128, T], BF16, name="xg", align_bytes=64)
+            words = t[:].rearrange("p v g r e -> p (v g r e)").bitcast(F32)
+            for v in range(2):
+                nc.scalar.copy(
+                    out=words[:, 512 * v : 512 * (v + 1)].rearrange("p (g r u) -> p g r u", g=G, u=2),
+                    in_=xs[s, v][:].rearrange("p g u r -> p g r u"),
+                )
+            xg[s] = t
+
+        def quantize_f(s):
+            cw = cp.tile([128, 2 * G * 128], U32, name="f_codes", align_bytes=64)
+            sc = cp.tile([128, 2 * G * 128], U8, name="f_scales", align_bytes=64)
+            nc.vector.quantize_mx(out=cw[:].bitcast(FP8X4), scales=sc[:], in_=xg[s][:].rearrange("p v g r e -> p (v g r e)"))
+            codes[s] = (cw, sc)
+
+        def split4(ap):
+            return ap.rearrange("p (c i t) -> p c t i", i=4, t=T)
+
+        def weighted(s, v):
+            if v == 0:
+                g_t[s] = gp.tile([128, 2, T, D // T], F32, name="g_pair")
+            k = 2 * (s % PAIRS) + v
+            pt = s // PAIRS
+            nc.vector.tensor_scalar(
+                out=g_t[s][:, v, :, :].rearrange("p t (c i) -> p c t i", i=4), in0=split4(f_pairs[s][:, v, :]),
+                scalar1=om[:, k, pt : pt + 1], scalar2=None, op0=ALU.mult,
+            )
+
+        def squared(s, v):
+            if v == 0:
+                q_t[s] = qp.tile([128, 2, T, D // T], F32, name="q_pair")
+            k = 2 * (s % PAIRS) + v
+            pt = s // PAIRS
+            nc.scalar.activation(
+                q_t[s][:, v, :, :].rearrange("p t (c i) -> p c t i", i=4), split4(f_pairs[s][:, v, :]),
+                ACT.Square, scale=rt[:, k, pt : pt + 1],
+            )
+
+        def sum_bank(pt, k):
+            src = g_t if k < 2 else q_t
+            g = k % 2
+            acc = ps_a.tile([128, T, PT], F32, name="acc")
+            for t in range(T):
+                for v in range(V):
+                    nc.tensor.matmul(
+                        acc[:, t, :], lhsT=src[PAIRS * pt + v // 2][:, v % 2, t, g * 128 : (g + 1) * 128], rhs=ident[:],
+                        start=(v == 0), stop=(v == V - 1), is_transpose=True,
+                    )
+            bank[pt, k] = acc
+
+        def stat_first(pt, k):
+            acc = bank[pt, k]
+            g = k % 2
+            if k == 0:
+                ab[pt] = sp.tile([128, 2, G, PT, T], BF16, name="ab", align_bytes=64)
+            if k < 2:
+                nc.vector.tensor_tensor(
+                    out=ab[pt][:, 0, g, :, :], in0=acc[:].rearrange("d t p -> d p t"),
+                    in1=gmv[:, g, :].unsqueeze(1).to_broadcast([128, PT, T]), op=ALU.mult,
+                )
+            else:
+                var_t[pt, g] = sp.tile([128, T, PT], F32, name="var")
+                nc.vector.tensor_tensor(out=var_t[pt, g][:], in0=acc[:], in1=musq[pt, g][:], op=ALU.subtract)
+
+        def stat_second(pt, k):
+            g = k % 2
+            if k < 2:
+                musq[pt, g] = sp.tile([128, T, PT], F32, name="musq")
+                nc.scalar.activation(musq[pt, g][:], bank[pt, k][:], ACT.Square)
+            else:
+                nc.vector.tensor_tensor(
+                    out=ab[pt][:, 1, g, :, :], in0=var_t[pt, g][:].rearrange("d t p -> d p t"),
+                    in1=gvt[:, g, :].unsqueeze(1).to_broadcast([128, PT, T]), op=ALU.mult,
+                )
+
+        def quantize_ab(pt):
+            cw = sp.tile([128, 2 * G * PT], U32, name="ab_codes", align_bytes=64)
+            sc = sp.tile([128, 2 * G * PT], U8, name="ab_scales", align_bytes=64)
+            nc.vector.quantize_mx(out=cw[:].bitcast(FP8X4), scales=sc[:], in_=ab[pt][:].rearrange("d x g p t -> d (x g p t)"))
+            abc[pt] = (cw, sc)
+
+        def product(acc, terms):
+            n = len(terms) * G
+            for j in range(n):
+                lhs, nm, first = terms[j // G]
+                g = j % G
+                cols = slice((first + g) * 128, (first + g + 1) * 128)
+                nc.tensor.matmul_mx(
+                    out=acc[:], lhsT=lhs[0][:, cols].bitcast(FP8X4), lhsT_scale=lhs[1][:, cols],
+                    rhs=codes_w[nm][:, g, :].bitcast(FP8X4), rhs_scale=scales_w[nm][:, g, :],
+                    start=(j == 0), stop=(j == n - 1),
+                )
+
+        def c_product(pt):
+            acc = ps_m.tile([128, H], F32, name="mm")
+            product(acc, ((abc[pt], "wm", 0), (abc[pt], "wv", G)))
+            c_ps[pt] = acc
+
+        def c_copy(pt):
+            c_sb[pt] = sp.tile([128, H], F32, name="c_sb")
+            nc.scalar.copy(out=c_sb[pt][:], in_=c_ps[pt][:])
+
+        def f_product(n):
+            for v in range(2):
+                if n in WITH_C:
+                    acc = ps_a.tile([128, H], F32, name="acc")
+                    product(acc, ((codes[n], "wf", v * G), (abc[n // PAIRS], "wm", 0), (abc[n // PAIRS], "wv", G)))
+                else:
+                    acc = ps_m.tile([128, H], F32, name="mm")
+                    product(acc, ((codes[n], "wf", v * G),))
+                mm[n, v] = acc
+
+        def add_c(n, v):
+            if v == 0:
+                e_t[n] = ep.tile([128, 2, H], F32, name="e", tag="e", align_bytes=64)
+            nc.vector.tensor_tensor(out=e_t[n][:, v, :], in0=mm[n, v][:], in1=c_sb[n // PAIRS][:], op=ALU.add)
+
+        def clamp(n):
+            m_t[n] = ep.tile([128, 2, H], F32, name="m", tag="m", align_bytes=64)
+            if n not in WITH_C and n not in BY_RELU:
+                nc.vector.tensor_scalar(out=m_t[n][:], in0=e_t[n][:], scalar1=0.0, scalar2=None, op0=ALU.min)
+
+        def exponential(n):
+            if n in WITH_C:
+                for v in range(2):
+                    nc.scalar.activation(m_t[n][:, v, :], mm[n, v][:], ACT.Relu, scale=-1.0)
+                nc.scalar.activation(m_t[n][:], m_t[n][:], ACT.Exp, scale=-1.0)
+            elif n in BY_RELU:
+                nc.scalar.activation(m_t[n][:], e_t[n][:], ACT.Relu, scale=-1.0)
+                nc.scalar.activation(m_t[n][:], m_t[n][:], ACT.Exp, scale=-1.0)
+            else:
+                nc.scalar.activation(m_t[n][:], m_t[n][:], ACT.Exp)
+
+        def finish(n):
+            if n in WITH_C:
+                for v in range(2):
+                    nc.vector.scalar_tensor_tensor(
+                        out=m_t[n][:, v, :], in0=m_t[n][:, v, :], scalar=-1.0, in1=mm[n, v][:], op0=ALU.add, op1=ALU.max
+                    )
+            else:
+                nc.vector.scalar_tensor_tensor(out=m_t[n][:], in0=m_t[n][:], scalar=-1.0, in1=e_t[n][:], op0=ALU.add, op1=ALU.max)
+            p0 = (n // PAIRS) * PT
+            v0 = 2 * (n % PAIRS)
+            nc.sync.dma_start(out=out[v0 : v0 + 2, p0 : p0 + PT, :].rearrange("v p h -> p v h"), in_=m_t[n][:])
+
+        f_pairs[1] = load_pair(1)
+        raws = {}
+        grps = {}
+        raws["wf", 0] = load_weight(wf, 0)
+        f_pairs[2] = load_pair(2)
+        raws["wf", 1] = load_weight(wf, 1)
+
+        with tc.manual_schedule():
+            for s in range(A_STEPS + LAG_E + 1):
+                n = s - LAG_E
+                has_a = s < A_STEPS
+                has_n = 0 <= n < A_STEPS
+                b = s - LAG_BANK
+                has_b = 0 <= b < NP * 4
+                done = b - 1
+                has_done = 0 <= done < NP * 4
+                cs = s - LAG_C
+                has_c = cs >= 0 and cs % 4 == 0 and cs // 4 < NP
+
+                if s + 3 < A_STEPS:
+                    f_pairs[s + 3] = load_pair(s + 3)
+                if s == 1:
+                    raws["wm", 0] = load_weight(wm, 0)
+                if s == 2:
+                    raws["wm", 1] = load_weight(wm, 1)
+                    nc.sync.dma_start(out=wv8[:], in_=wv_bytes.rearrange("(g p t) n -> p g (t n)", p=128, t=T))
+                if has_a:
+                    transposes(s)
+                if has_c:
+                    c_product(cs // 4)
+                if 0 <= n + 1 < A_STEPS:
+                    f_product(n + 1)
+                if has_n and n not in WITH_C:
+                    add_c(n, 0)
+                    add_c(n, 1)
+                if has_a:
+                    weighted(s, 0)
+                    squared(s, 0)
+                if has_n:
+                    clamp(n)
+                if has_done:
+                    stat_first(done // 4, done % 4)
+                if 0 <= n - 1 < A_STEPS:
+                    finish(n - 1)
+                if has_a:
+                    weighted(s, 1)
+                    squared(s, 1)
+                if has_b:
+                    sum_bank(b // 4, b % 4)
+                if has_done:
+                    stat_second(done // 4, done % 4)
+                if has_n:
+                    exponential(n)
+                if has_c:
+                    c_copy(cs // 4)
+                if 1 <= s <= A_STEPS:
+                    quantize_f(s - 1)
+                if has_a:
+                    evacuate(s)
+                if has_done and done % 4 == 3:
+                    quantize_ab(done // 4)
+                if s <= 5:
+                    key = (("wf", "wm", "wv")[s // 2], s % 2)
+                    if key[0] == "wv":
+                        raws[key] = widen_wv(key[1])
+                    grps[key] = interleave(raws[key])
+                if 1 <= s <= 6:
+                    key = (("wf", "wm", "wv")[(s - 1) // 2], (s - 1) % 2)
+                    quantize_weight(grps[key], key[0], key[1])

@@ -26,6 +26,7 @@ LAG_BANK = 3
 LAG_C = 8
 WITH_C = (27, 29, 31)
 BY_RELU = tuple(n for n in range(A_STEPS) if n >= 24 or n % 5 in (1, 3))
+WARM_FROM = 2
 LAG_E = 9
 
 
@@ -143,25 +144,27 @@ def tile_ibrnetviewstatisticsmixer_t_kernel(tc, f, lw, gm, gv, wf, wm, wv_bytes,
         m_t = {}
         var_t = {}
 
-        def transposes(s):
+        def transposes(s, v):
             words = f_pairs[s][:].rearrange("p v d -> p (v d)").bitcast(F32)
-            for v in range(2):
-                xt = ps_x.tile([128, 2, 2, 128], F32, name="xt")
-                for g in range(G):
-                    for u in range(2):
-                        w0 = 512 * v + 256 * g
-                        nc.tensor.transpose(xt[:, g, u, :], words[:, w0 + u : w0 + 256 : 2], ident[:])
-                xs[s, v] = xt
+            xt = ps_x.tile([128, 2, 2, 128], F32, name="xt")
+            for g in range(G):
+                for u in range(2):
+                    w0 = 512 * v + 256 * g
+                    nc.tensor.transpose(xt[:, g, u, :], words[:, w0 + u : w0 + 256 : 2], ident[:])
+            xs[s, v] = xt
 
-        def evacuate(s):
-            t = xp.tile([128, 2, G, 128, T], BF16, name="xg", align_bytes=64)
-            words = t[:].rearrange("p v g r e -> p (v g r e)").bitcast(F32)
-            for v in range(2):
-                nc.scalar.copy(
-                    out=words[:, 512 * v : 512 * (v + 1)].rearrange("p (g r u) -> p g r u", g=G, u=2),
-                    in_=xs[s, v][:].rearrange("p g u r -> p g r u"),
-                )
-            xg[s] = t
+        def evacuate(s, v):
+            if v == 0:
+                xg[s] = xp.tile([128, 2, G, 128, T], BF16, name="xg", align_bytes=64)
+            words = xg[s][:].rearrange("p v g r e -> p (v g r e)").bitcast(F32)
+            nc.scalar.copy(
+                out=words[:, 512 * v : 512 * (v + 1)].rearrange("p (g r u) -> p g r u", g=G, u=2),
+                in_=xs[s, v][:].rearrange("p g u r -> p g r u"),
+            )
+
+        def warm(s):
+            t = ps_m.tile([128, H], F32, name="mm")
+            nc.tensor.matmul(t[:], lhsT=f_pairs[s][:, 0, 0:128], rhs=f_pairs[s][:, 0, 0:H], start=True, stop=True)
 
         def quantize_f(s):
             cw = cp.tile([128, 2 * G * 128], U32, name="f_codes", align_bytes=64)
@@ -192,17 +195,18 @@ def tile_ibrnetviewstatisticsmixer_t_kernel(tc, f, lw, gm, gv, wf, wm, wv_bytes,
                 ACT.Square, scale=rt[:, k, pt : pt + 1],
             )
 
-        def sum_bank(pt, k):
+        def sum_bank(pt, k, half):
             src = g_t if k < 2 else q_t
             g = k % 2
-            acc = ps_a.tile([128, T, PT], F32, name="acc")
-            for t in range(T):
+            if half == 0:
+                bank[pt, k] = ps_a.tile([128, T, PT], F32, name="acc")
+            acc = bank[pt, k]
+            for t in (2 * half, 2 * half + 1):
                 for v in range(V):
                     nc.tensor.matmul(
                         acc[:, t, :], lhsT=src[PAIRS * pt + v // 2][:, v % 2, t, g * 128 : (g + 1) * 128], rhs=ident[:],
                         start=(v == 0), stop=(v == V - 1), is_transpose=True,
                     )
-            bank[pt, k] = acc
 
         def stat_first(pt, k):
             acc = bank[pt, k]
@@ -256,15 +260,14 @@ def tile_ibrnetviewstatisticsmixer_t_kernel(tc, f, lw, gm, gv, wf, wm, wv_bytes,
             c_sb[pt] = sp.tile([128, H], F32, name="c_sb")
             nc.scalar.copy(out=c_sb[pt][:], in_=c_ps[pt][:])
 
-        def f_product(n):
-            for v in range(2):
-                if n in WITH_C:
-                    acc = ps_a.tile([128, H], F32, name="acc")
-                    product(acc, ((codes[n], "wf", v * G), (abc[n // PAIRS], "wm", 0), (abc[n // PAIRS], "wv", G)))
-                else:
-                    acc = ps_m.tile([128, H], F32, name="mm")
-                    product(acc, ((codes[n], "wf", v * G),))
-                mm[n, v] = acc
+        def f_product(n, v):
+            if n in WITH_C:
+                acc = ps_a.tile([128, H], F32, name="acc")
+                product(acc, ((codes[n], "wf", v * G), (abc[n // PAIRS], "wm", 0), (abc[n // PAIRS], "wv", G)))
+            else:
+                acc = ps_m.tile([128, H], F32, name="mm")
+                product(acc, ((codes[n], "wf", v * G),))
+            mm[n, v] = acc
 
         def add_c(n, v):
             if v == 0:
@@ -311,6 +314,7 @@ def tile_ibrnetviewstatisticsmixer_t_kernel(tc, f, lw, gm, gv, wf, wm, wv_bytes,
                 n = s - LAG_E
                 has_a = s < A_STEPS
                 has_n = 0 <= n < A_STEPS
+                has_next = 0 <= n + 1 < A_STEPS
                 b = s - LAG_BANK
                 has_b = 0 <= b < NP * 4
                 done = b - 1
@@ -326,11 +330,15 @@ def tile_ibrnetviewstatisticsmixer_t_kernel(tc, f, lw, gm, gv, wf, wm, wv_bytes,
                     raws["wm", 1] = load_weight(wm, 1)
                     nc.sync.dma_start(out=wv8[:], in_=wv_bytes.rearrange("(g p t) n -> p g (t n)", p=128, t=T))
                 if has_a:
-                    transposes(s)
+                    transposes(s, 0)
                 if has_c:
                     c_product(cs // 4)
-                if 0 <= n + 1 < A_STEPS:
-                    f_product(n + 1)
+                if has_next:
+                    f_product(n + 1, 0)
+                if WARM_FROM <= s < LAG_E - 1:
+                    warm(s)
+                if has_done:
+                    sum_bank(done // 4, done % 4, 1)
                 if has_n and n not in WITH_C:
                     add_c(n, 0)
                     add_c(n, 1)
@@ -339,25 +347,33 @@ def tile_ibrnetviewstatisticsmixer_t_kernel(tc, f, lw, gm, gv, wf, wm, wv_bytes,
                     squared(s, 0)
                 if has_n:
                     clamp(n)
-                if has_done:
-                    stat_first(done // 4, done % 4)
                 if 0 <= n - 1 < A_STEPS:
                     finish(n - 1)
                 if has_a:
                     weighted(s, 1)
                     squared(s, 1)
-                if has_b:
-                    sum_bank(b // 4, b % 4)
                 if has_done:
-                    stat_second(done // 4, done % 4)
+                    stat_first(done // 4, done % 4)
+                if has_a:
+                    transposes(s, 1)
+                if has_next:
+                    f_product(n + 1, 1)
+                if WARM_FROM <= s < LAG_E - 1:
+                    warm(s)
+                if has_b:
+                    sum_bank(b // 4, b % 4, 0)
                 if has_n:
                     exponential(n)
-                if has_c:
-                    c_copy(cs // 4)
                 if 1 <= s <= A_STEPS:
                     quantize_f(s - 1)
+                if has_c:
+                    c_copy(cs // 4)
                 if has_a:
-                    evacuate(s)
+                    evacuate(s, 0)
+                if has_done:
+                    stat_second(done // 4, done % 4)
+                if has_a:
+                    evacuate(s, 1)
                 if has_done and done % 4 == 3:
                     quantize_ab(done // 4)
                 if s <= 5:

@@ -24,9 +24,16 @@ PAIRS = V // 2
 A_STEPS = NP * PAIRS
 LAG_BANK = 3
 LAG_C = 8
-WITH_C = (27, 29, 31)
-BY_RELU = tuple(n for n in range(A_STEPS) if n >= 24 or n % 5 in (1, 3))
-WARM_FROM = 2
+WITH_C = (28,30)
+BY_RELU = tuple(n for n in range(A_STEPS) if n>=24 or n%2==1)
+HEAD_FROM, HEAD_TO, HEAD_N, STEADY = 3, 8, (2, 2), (0, 1)
+
+
+def dummies(s, v):
+    return HEAD_N[v] if HEAD_FROM <= s < HEAD_TO else STEADY[v] if s >= HEAD_TO else 0
+
+
+PRE_ADDED = (0,2)
 LAG_E = 9
 
 
@@ -147,6 +154,10 @@ def tile_ibrnetviewstatisticsmixer_t_kernel(tc, f, lw, gm, gv, wf, wm, wv_bytes,
         def transposes(s, v):
             words = f_pairs[s][:].rearrange("p v d -> p (v d)").bitcast(F32)
             xt = ps_x.tile([128, 2, 2, 128], F32, name="xt")
+            for j in range(dummies(s, v)):
+                nc.tensor.matmul(
+                    xt[:].rearrange("p g u r -> p (g u r)"), lhsT=f_pairs[s][:, v, 0:128], rhs=f_pairs[s][:, v, 0:H], start=True, stop=True
+                )
             for g in range(G):
                 for u in range(2):
                     w0 = 512 * v + 256 * g
@@ -162,10 +173,6 @@ def tile_ibrnetviewstatisticsmixer_t_kernel(tc, f, lw, gm, gv, wf, wm, wv_bytes,
                 in_=xs[s, v][:].rearrange("p g u r -> p g r u"),
             )
 
-        def warm(s):
-            t = ps_m.tile([128, H], F32, name="mm")
-            nc.tensor.matmul(t[:], lhsT=f_pairs[s][:, 0, 0:128], rhs=f_pairs[s][:, 0, 0:H], start=True, stop=True)
-
         def quantize_f(s):
             cw = cp.tile([128, 2 * G * 128], U32, name="f_codes", align_bytes=64)
             sc = cp.tile([128, 2 * G * 128], U8, name="f_scales", align_bytes=64)
@@ -180,6 +187,12 @@ def tile_ibrnetviewstatisticsmixer_t_kernel(tc, f, lw, gm, gv, wf, wm, wv_bytes,
                 g_t[s] = gp.tile([128, 2, T, D // T], F32, name="g_pair")
             k = 2 * (s % PAIRS) + v
             pt = s // PAIRS
+            if v == 1 and s % PAIRS in PRE_ADDED:
+                nc.vector.scalar_tensor_tensor(
+                    out=g_t[s][:, 0, :, :], in0=f_pairs[s][:, v, :].rearrange("p (i t) -> p t i", t=T),
+                    scalar=om[:, k, pt : pt + 1], in1=g_t[s][:, 0, :, :], op0=ALU.mult, op1=ALU.add,
+                )
+                return
             nc.vector.tensor_scalar(
                 out=g_t[s][:, v, :, :].rearrange("p t (c i) -> p c t i", i=4), in0=split4(f_pairs[s][:, v, :]),
                 scalar1=om[:, k, pt : pt + 1], scalar2=None, op0=ALU.mult,
@@ -201,11 +214,12 @@ def tile_ibrnetviewstatisticsmixer_t_kernel(tc, f, lw, gm, gv, wf, wm, wv_bytes,
             if half == 0:
                 bank[pt, k] = ps_a.tile([128, T, PT], F32, name="acc")
             acc = bank[pt, k]
+            views = [v for v in range(V) if k >= 2 or v % 2 == 0 or v // 2 not in PRE_ADDED]
             for t in (2 * half, 2 * half + 1):
-                for v in range(V):
+                for v in views:
                     nc.tensor.matmul(
                         acc[:, t, :], lhsT=src[PAIRS * pt + v // 2][:, v % 2, t, g * 128 : (g + 1) * 128], rhs=ident[:],
-                        start=(v == 0), stop=(v == V - 1), is_transpose=True,
+                        start=(v == views[0]), stop=(v == views[-1]), is_transpose=True,
                     )
 
         def stat_first(pt, k):
@@ -309,78 +323,79 @@ def tile_ibrnetviewstatisticsmixer_t_kernel(tc, f, lw, gm, gv, wf, wm, wv_bytes,
         f_pairs[2] = load_pair(2)
         raws["wf", 1] = load_weight(wf, 1)
 
-        with tc.manual_schedule():
-            for s in range(A_STEPS + LAG_E + 1):
-                n = s - LAG_E
-                has_a = s < A_STEPS
-                has_n = 0 <= n < A_STEPS
-                has_next = 0 <= n + 1 < A_STEPS
-                b = s - LAG_BANK
-                has_b = 0 <= b < NP * 4
-                done = b - 1
-                has_done = 0 <= done < NP * 4
-                cs = s - LAG_C
-                has_c = cs >= 0 and cs % 4 == 0 and cs // 4 < NP
+        def load_late(i):
+            if i < 2:
+                raws["wm", i] = load_weight(wm, i)
+            else:
+                nc.sync.dma_start(out=wv8[:], in_=wv_bytes.rearrange("(g p t) n -> p g (t n)", p=128, t=T))
 
-                if s + 3 < A_STEPS:
-                    f_pairs[s + 3] = load_pair(s + 3)
-                if s == 1:
-                    raws["wm", 0] = load_weight(wm, 0)
-                if s == 2:
-                    raws["wm", 1] = load_weight(wm, 1)
-                    nc.sync.dma_start(out=wv8[:], in_=wv_bytes.rearrange("(g p t) n -> p g (t n)", p=128, t=T))
-                if has_a:
-                    transposes(s, 0)
-                if has_c:
-                    c_product(cs // 4)
-                if has_next:
-                    f_product(n + 1, 0)
-                if WARM_FROM <= s < LAG_E - 1:
-                    warm(s)
-                if has_done:
-                    sum_bank(done // 4, done % 4, 1)
-                if has_n and n not in WITH_C:
-                    add_c(n, 0)
-                    add_c(n, 1)
-                if has_a:
-                    weighted(s, 0)
-                    squared(s, 0)
-                if has_n:
-                    clamp(n)
-                if 0 <= n - 1 < A_STEPS:
-                    finish(n - 1)
-                if has_a:
-                    weighted(s, 1)
-                    squared(s, 1)
-                if has_done:
-                    stat_first(done // 4, done % 4)
-                if has_a:
-                    transposes(s, 1)
-                if has_next:
-                    f_product(n + 1, 1)
-                if WARM_FROM <= s < LAG_E - 1:
-                    warm(s)
-                if has_b:
-                    sum_bank(b // 4, b % 4, 0)
-                if has_n:
-                    exponential(n)
-                if 1 <= s <= A_STEPS:
-                    quantize_f(s - 1)
-                if has_c:
-                    c_copy(cs // 4)
-                if has_a:
-                    evacuate(s, 0)
-                if has_done:
-                    stat_second(done // 4, done % 4)
-                if has_a:
-                    evacuate(s, 1)
-                if has_done and done % 4 == 3:
-                    quantize_ab(done // 4)
-                if s <= 5:
-                    key = (("wf", "wm", "wv")[s // 2], s % 2)
-                    if key[0] == "wv":
-                        raws[key] = widen_wv(key[1])
-                    grps[key] = interleave(raws[key])
-                if 1 <= s <= 6:
-                    key = (("wf", "wm", "wv")[(s - 1) // 2], (s - 1) % 2)
-                    quantize_weight(grps[key], key[0], key[1])
+        def lay(i):
+            key = (("wf", "wm", "wv")[i // 2], i % 2)
+            if key[0] == "wv":
+                raws[key] = widen_wv(key[1])
+            grps[key] = interleave(raws[key])
+
+        def quant_w(i):
+            key = (("wf", "wm", "wv")[i // 2], i % 2)
+            quantize_weight(grps[key], key[0], key[1])
+
+        def adds(n, v):
+            if n not in WITH_C:
+                add_c(n, v)
+
+        with tc.manual_schedule():
+            for s in range(A_STEPS + 12):
+                if 0 <= s - 11 < A_STEPS and (s - 11) % 4 == 0:
+                    c_copy((s - 11) // 4)
+                if 0 <= s - 4 < A_STEPS:
+                    quantize_f(s - 4)
+                if 0 <= s - 10 < A_STEPS and (s - 10) % 4 == 0:
+                    c_product((s - 10) // 4)
+                if 0 <= s - 4 < 6:
+                    quant_w(s - 4)
+                if 0 <= s - 10 < A_STEPS:
+                    f_product(s - 10, 0)
+                if 3 <= s + 2 < A_STEPS:
+                    f_pairs[(s + 2)] = load_pair(s + 2)
+                if 0 <= s - 11 < A_STEPS:
+                    adds(s - 11, 0)
+                if 0 <= s - 11 < A_STEPS:
+                    adds(s - 11, 1)
+                if 0 <= s - 2 < A_STEPS:
+                    weighted(s - 2, 1)
+                if 0 <= s - 2 < A_STEPS:
+                    squared(s - 2, 0)
+                if 0 <= s - 6 < 4 * NP:
+                    sum_bank((s - 6) // 4, (s - 6) % 4, 1)
+                if 0 <= s - 12 < A_STEPS:
+                    exponential(s - 12)
+                if 0 <= s - 11 < A_STEPS:
+                    clamp(s - 11)
+                if 0 <= s - 6 < 4 * NP:
+                    stat_first((s - 6) // 4, (s - 6) % 4)
+                if 0 <= s - 2 < A_STEPS:
+                    transposes(s - 2, 1)
+                if 0 <= s < 3:
+                    load_late(s)
+                if 0 <= s - 2 < 6:
+                    lay(s - 2)
+                if 0 <= s - 12 < A_STEPS:
+                    finish(s - 12)
+                if 0 <= s - 10 < A_STEPS:
+                    f_product(s - 10, 1)
+                if 0 <= s - 1 < A_STEPS:
+                    transposes(s - 1, 0)
+                if 0 <= s - 2 < A_STEPS:
+                    evacuate(s - 2, 0)
+                if 0 <= s - 2 < A_STEPS:
+                    squared(s - 2, 1)
+                if 0 <= s - 2 < A_STEPS:
+                    evacuate(s - 2, 1)
+                if 0 <= s - 5 < 4 * NP:
+                    sum_bank((s - 5) // 4, (s - 5) % 4, 0)
+                if 0 <= s - 6 < 4 * NP:
+                    stat_second((s - 6) // 4, (s - 6) % 4)
+                if 0 <= s - 9 < A_STEPS and (s - 9) % 4 == 0:
+                    quantize_ab((s - 9) // 4)
+                if 0 <= s - 1 < A_STEPS:
+                    weighted(s - 1, 0)

@@ -24,16 +24,16 @@ PAIRS = V // 2
 A_STEPS = NP * PAIRS
 LAG_BANK = 3
 LAG_C = 8
-WITH_C = (28,30)
-BY_RELU = tuple(n for n in range(A_STEPS) if n>=24 or n%2==1)
-HEAD_FROM, HEAD_TO, HEAD_N, STEADY = 3, 8, (2, 2), (0, 1)
+WITH_C = (28, 30)
+BY_RELU = tuple(n for n in range(A_STEPS) if n >= 24)
+HEAD_FROM, HEAD_TO, HEAD_N, STEADY = 3, 8, (2, 2), (0, 0)
 
 
 def dummies(s, v):
     return HEAD_N[v] if HEAD_FROM <= s < HEAD_TO else STEADY[v] if s >= HEAD_TO else 0
 
 
-PRE_ADDED = (0,2)
+PRE_ADDED = ()
 LAG_E = 9
 
 
@@ -344,58 +344,58 @@ def tile_ibrnetviewstatisticsmixer_t_kernel(tc, f, lw, gm, gv, wf, wm, wv_bytes,
                 add_c(n, v)
 
         with tc.manual_schedule():
-            for s in range(A_STEPS + 12):
-                if 0 <= s - 11 < A_STEPS and (s - 11) % 4 == 0:
-                    c_copy((s - 11) // 4)
-                if 0 <= s - 4 < A_STEPS:
-                    quantize_f(s - 4)
-                if 0 <= s - 10 < A_STEPS and (s - 10) % 4 == 0:
-                    c_product((s - 10) // 4)
-                if 0 <= s - 4 < 6:
-                    quant_w(s - 4)
-                if 0 <= s - 10 < A_STEPS:
-                    f_product(s - 10, 0)
-                if 3 <= s + 2 < A_STEPS:
-                    f_pairs[(s + 2)] = load_pair(s + 2)
-                if 0 <= s - 11 < A_STEPS:
-                    adds(s - 11, 0)
-                if 0 <= s - 11 < A_STEPS:
-                    adds(s - 11, 1)
-                if 0 <= s - 2 < A_STEPS:
-                    weighted(s - 2, 1)
-                if 0 <= s - 2 < A_STEPS:
-                    squared(s - 2, 0)
-                if 0 <= s - 6 < 4 * NP:
-                    sum_bank((s - 6) // 4, (s - 6) % 4, 1)
-                if 0 <= s - 12 < A_STEPS:
-                    exponential(s - 12)
-                if 0 <= s - 11 < A_STEPS:
-                    clamp(s - 11)
-                if 0 <= s - 6 < 4 * NP:
-                    stat_first((s - 6) // 4, (s - 6) % 4)
-                if 0 <= s - 2 < A_STEPS:
-                    transposes(s - 2, 1)
-                if 0 <= s < 3:
-                    load_late(s)
-                if 0 <= s - 2 < 6:
-                    lay(s - 2)
-                if 0 <= s - 12 < A_STEPS:
-                    finish(s - 12)
-                if 0 <= s - 10 < A_STEPS:
-                    f_product(s - 10, 1)
-                if 0 <= s - 1 < A_STEPS:
-                    transposes(s - 1, 0)
-                if 0 <= s - 2 < A_STEPS:
-                    evacuate(s - 2, 0)
-                if 0 <= s - 2 < A_STEPS:
-                    squared(s - 2, 1)
-                if 0 <= s - 2 < A_STEPS:
-                    evacuate(s - 2, 1)
-                if 0 <= s - 5 < 4 * NP:
-                    sum_bank((s - 5) // 4, (s - 5) % 4, 0)
-                if 0 <= s - 6 < 4 * NP:
-                    stat_second((s - 6) // 4, (s - 6) % 4)
-                if 0 <= s - 9 < A_STEPS and (s - 9) % 4 == 0:
-                    quantize_ab((s - 9) // 4)
-                if 0 <= s - 1 < A_STEPS:
-                    weighted(s - 1, 0)
+            for s in range(A_STEPS + 17):
+                if 0 <= s - 4 < 3:
+                    load_late(s - 4)
+                if 0 <= s - 8 < A_STEPS:
+                    evacuate(s - 8, 1)
+                if 0 <= s - 16 < A_STEPS:
+                    adds(s - 16, 0)
+                if 0 <= s - 8 < 6:
+                    quant_w(s - 8)
+                if 0 <= s - 16 < A_STEPS:
+                    adds(s - 16, 1)
+                if 0 <= s - 9 < A_STEPS:
+                    quantize_f(s - 9)
+                if 0 <= s - 7 < 6:
+                    lay(s - 7)
+                if 0 <= s - 7 < A_STEPS:
+                    evacuate(s - 7, 0)
+                if 0 <= s - 15 < A_STEPS and (s - 15) % 4 == 0:
+                    c_copy((s - 15) // 4)
+                if 0 <= s - 16 < A_STEPS:
+                    clamp(s - 16)
+                if 0 <= s - 11 < 4 * NP:
+                    stat_first((s - 11) // 4, (s - 11) % 4)
+                if 0 <= s - 16 < A_STEPS:
+                    exponential(s - 16)
+                if 3 <= s - 4 < A_STEPS:
+                    f_pairs[(s - 4)] = load_pair(s - 4)
+                if 0 <= s - 15 < A_STEPS:
+                    f_product(s - 15, 0)
+                if 0 <= s - 7 < A_STEPS:
+                    squared(s - 7, 0)
+                if 0 <= s - 6 < A_STEPS:
+                    weighted(s - 6, 0)
+                if 0 <= s - 7 < A_STEPS:
+                    transposes(s - 7, 1)
+                if 0 <= s - 11 < 4 * NP:
+                    stat_second((s - 11) // 4, (s - 11) % 4)
+                if 0 <= s - 10 < 4 * NP:
+                    sum_bank((s - 10) // 4, (s - 10) % 4, 0)
+                if 0 <= s - 15 < A_STEPS:
+                    f_product(s - 15, 1)
+                if 0 <= s - 7 < A_STEPS:
+                    squared(s - 7, 1)
+                if 0 <= s - 6 < A_STEPS:
+                    weighted(s - 6, 1)
+                if 0 <= s - 14 < A_STEPS and (s - 14) % 4 == 0:
+                    quantize_ab((s - 14) // 4)
+                if 0 <= s - 6 < A_STEPS:
+                    transposes(s - 6, 0)
+                if 0 <= s - 17 < A_STEPS:
+                    finish(s - 17)
+                if 0 <= s - 10 < 4 * NP:
+                    sum_bank((s - 10) // 4, (s - 10) % 4, 1)
+                if 0 <= s - 14 < A_STEPS and (s - 14) % 4 == 0:
+                    c_product((s - 14) // 4)

from contextlib import ExitStack

import concourse.mybir as mybir
from concourse.masks import make_identity

V, P, D, H = 8, 1024, 1024, 512
FLOPS = 2 * V * P * D * H + 2 * (2 * P * D * H)

F32 = mybir.dt.float32
BF16 = mybir.dt.bfloat16
U32 = mybir.dt.uint32
U8 = mybir.dt.uint8
FP8 = mybir.dt.float8_e4m3fn
FP8X4 = mybir.dt.float8_e4m3fn_x4
ALU = mybir.AluOpType
ACT = mybir.ActivationFunctionType
AX = mybir.AxisListType

PT = 128
NP = P // PT
G = D // 512
T = 4
PAIRS = V // 2
A_STEPS = NP * PAIRS
LAG_BANK = 3
LAG_C = 8
WITH_C = (28, 30)
BY_RELU = tuple(n for n in range(A_STEPS) if n >= 24)
HEAD_FROM, HEAD_TO, HEAD_N, STEADY = 3, 8, (2, 2), (0, 0)


def dummies(s, v):
    return HEAD_N[v] if HEAD_FROM <= s < HEAD_TO else STEADY[v] if s >= HEAD_TO else 0


PRE_ADDED = ()
LAG_E = 9


def tile_ibrnetviewstatisticsmixer_t_kernel(tc, f, lw, gm, gv, wf, wm, wv_bytes, wv_scale, out):
    nc = tc.nc
    with ExitStack() as ctx:
        keep = ctx.enter_context(tc.tile_pool(name="keep", bufs=1))
        fp = ctx.enter_context(tc.tile_pool(name="fp", bufs=4))
        gp = ctx.enter_context(tc.tile_pool(name="gp", bufs=6))
        qp = ctx.enter_context(tc.tile_pool(name="qp", bufs=8))
        xp = ctx.enter_context(tc.tile_pool(name="xp", bufs=2))
        cp = ctx.enter_context(tc.tile_pool(name="cp", bufs=10))
        ep = ctx.enter_context(tc.tile_pool(name="ep", bufs=3))
        sp = ctx.enter_context(tc.tile_pool(name="sp", bufs=2))
        ps_x = ctx.enter_context(tc.psum_pool(name="ps_x", bufs=3))
        ps_a = ctx.enter_context(tc.psum_pool(name="ps_a", bufs=2))
        ps_m = ctx.enter_context(tc.psum_pool(name="ps_m", bufs=3))

        ident = keep.tile([128, 128], F32, name="ident")
        make_identity(nc, ident[:])

        def load_pair(s):
            p0 = (s // PAIRS) * PT
            v0 = 2 * (s % PAIRS)
            t = fp.tile([128, 2, D], BF16, name="f_pair", align_bytes=64)
            nc.sync.dma_start(out=t[:], in_=f[v0 : v0 + 2, p0 : p0 + PT, :].rearrange("v p d -> p v d"))
            return t

        f_pairs = {}

        lw_rows = keep.tile([128, 128], BF16, name="lw_rows")
        nc.vector.memset(lw_rows[64:128, :], 0.0)
        nc.sync.dma_start(out=lw_rows[0:64, :], in_=lw.rearrange("v (t p) -> (v t) p", p=PT))
        f_pairs[0] = load_pair(0)
        gmv = keep.tile([128, G, T], BF16, name="gmv")
        nc.sync.dma_start(out=gmv[:], in_=gm.rearrange("(g p t) -> p g t", p=128, t=T))
        gvt = keep.tile([128, G, T], BF16, name="gvt")
        nc.sync.dma_start(out=gvt[:], in_=gv.rearrange("(g p t) -> p g t", p=128, t=T))
        wsc = keep.tile([128, G, T], F32, name="wsc")
        nc.sync.dma_start(out=wsc[:], in_=wv_scale.rearrange("(g p t) o -> p g (t o)", p=128, t=T))

        lw_f = keep.tile([128, 128], F32, name="lw_f")
        nc.vector.tensor_copy(out=lw_f[:], in_=lw_rows[:])
        lw_t = ps_x.tile([128, 2, 2, 128], F32, name="xt")
        nc.tensor.transpose(lw_t[:, 0, 0, :], lw_f[:], ident[:])
        z = keep.tile([128, V, NP], F32, name="z")
        nc.vector.tensor_copy(out=z[:].rearrange("p v t -> p (v t)"), in_=lw_t[:, 0, 0, 0:64])
        mx = keep.tile([128, NP], F32, name="mx")
        nc.vector.reduce_max(mx[:], z[:].rearrange("p v t -> p t v"), axis=AX.X)
        zs = keep.tile([128, V, NP], F32, name="zs")
        nc.vector.tensor_tensor(out=zs[:], in0=z[:], in1=mx[:].unsqueeze(1).to_broadcast([128, V, NP]), op=ALU.subtract)
        om = keep.tile([128, V, NP], F32, name="om")
        rt = keep.tile([128, V, NP], F32, name="rt")
        nc.scalar.activation(om[:], zs[:], ACT.Exp)
        nc.scalar.activation(rt[:], zs[:], ACT.Exp, scale=0.5)
        tot = keep.tile([128, NP], F32, name="tot")
        nc.vector.reduce_sum(tot[:], om[:].rearrange("p v t -> p t v"), axis=AX.X)
        inv = keep.tile([128, NP], F32, name="inv")
        nc.vector.reciprocal(inv[:], tot[:])
        y0 = keep.tile([128, NP], F32, name="y0")
        nc.scalar.activation(y0[:], inv[:], ACT.Sqrt)
        y1 = keep.tile([128, NP], F32, name="y1")
        nc.vector.reciprocal(y1[:], y0[:])
        nc.vector.tensor_tensor(out=y1[:], in0=y1[:], in1=inv[:], op=ALU.mult)
        nc.vector.tensor_tensor(out=y1[:], in0=y1[:], in1=y0[:], op=ALU.add)
        nc.vector.tensor_scalar(out=y1[:], in0=y1[:], scalar1=0.5, scalar2=None, op0=ALU.mult)
        nc.vector.tensor_tensor(out=om[:], in0=om[:], in1=inv[:].unsqueeze(1).to_broadcast([128, V, NP]), op=ALU.mult)
        nc.vector.tensor_tensor(out=rt[:], in0=rt[:], in1=y1[:].unsqueeze(1).to_broadcast([128, V, NP]), op=ALU.mult)

        codes_w = {}
        scales_w = {}
        for nm in ("wf", "wm", "wv"):
            codes_w[nm] = keep.tile([128, G, H], U32, name="codes_" + nm, align_bytes=64)
            scales_w[nm] = keep.tile([128, G, H], U8, name="scales_" + nm, align_bytes=64)
        wv8 = keep.tile([128, G, T * H], U8, name="wv8")

        def load_weight(w, g):
            raw = ep.tile([128, T, H], BF16, name="raw", tag="e", align_bytes=64)
            nc.sync.dma_start(out=raw[:], in_=w.rearrange("(g p t) n -> g p t n", p=128, t=T)[g])
            return raw

        def widen_wv(g):
            raw = ep.tile([128, T, H], BF16, name="raw", tag="e", align_bytes=64)
            for t in range(T):
                nc.vector.tensor_scalar(
                    out=raw[:, t, :], in0=wv8[:, g, t * H : (t + 1) * H].bitcast(FP8), scalar1=wsc[:, g, t : t + 1], scalar2=None, op0=ALU.mult
                )
            return raw

        def interleave(raw):
            grp = ep.tile([128, H, T], BF16, name="grp", tag="m", align_bytes=64)
            nc.vector.tensor_copy(
                out=grp[:].rearrange("p (c i) t -> p c t i", i=4), in_=raw[:].rearrange("p t (c i) -> p c t i", i=4)
            )
            return grp

        def quantize_weight(grp, nm, g):
            nc.vector.quantize_mx(
                out=codes_w[nm][:, g, :].bitcast(FP8X4), scales=scales_w[nm][:, g, :], in_=grp[:].rearrange("p n t -> p (n t)")
            )

        xs = {}
        xg = {}
        codes = {}
        g_t = {}
        q_t = {}
        bank = {}
        musq = {}
        ab = {}
        abc = {}
        c_ps = {}
        c_sb = {}
        mm = {}
        e_t = {}
        m_t = {}
        var_t = {}

        def transposes(s, v):
            words = f_pairs[s][:].rearrange("p v d -> p (v d)").bitcast(F32)
            xt = ps_x.tile([128, 2, 2, 128], F32, name="xt")
            for j in range(dummies(s, v)):
                nc.tensor.matmul(
                    xt[:].rearrange("p g u r -> p (g u r)"), lhsT=f_pairs[s][:, v, 0:128], rhs=f_pairs[s][:, v, 0:H], start=True, stop=True
                )
            for g in range(G):
                for u in range(2):
                    w0 = 512 * v + 256 * g
                    nc.tensor.transpose(xt[:, g, u, :], words[:, w0 + u : w0 + 256 : 2], ident[:])
            xs[s, v] = xt

        def evacuate(s, v):
            if v == 0:
                xg[s] = xp.tile([128, 2, G, 128, T], BF16, name="xg", align_bytes=64)
            words = xg[s][:].rearrange("p v g r e -> p (v g r e)").bitcast(F32)
            nc.scalar.copy(
                out=words[:, 512 * v : 512 * (v + 1)].rearrange("p (g r u) -> p g r u", g=G, u=2),
                in_=xs[s, v][:].rearrange("p g u r -> p g r u"),
            )

        def quantize_f(s):
            cw = cp.tile([128, 2 * G * 128], U32, name="f_codes", align_bytes=64)
            sc = cp.tile([128, 2 * G * 128], U8, name="f_scales", align_bytes=64)
            nc.vector.quantize_mx(out=cw[:].bitcast(FP8X4), scales=sc[:], in_=xg[s][:].rearrange("p v g r e -> p (v g r e)"))
            codes[s] = (cw, sc)

        def split4(ap):
            return ap.rearrange("p (c i t) -> p c t i", i=4, t=T)

        def weighted(s, v):
            if v == 0:
                g_t[s] = gp.tile([128, 2, T, D // T], F32, name="g_pair")
            k = 2 * (s % PAIRS) + v
            pt = s // PAIRS
            if v == 1 and s % PAIRS in PRE_ADDED:
                nc.vector.scalar_tensor_tensor(
                    out=g_t[s][:, 0, :, :], in0=f_pairs[s][:, v, :].rearrange("p (i t) -> p t i", t=T),
                    scalar=om[:, k, pt : pt + 1], in1=g_t[s][:, 0, :, :], op0=ALU.mult, op1=ALU.add,
                )
                return
            nc.vector.tensor_scalar(
                out=g_t[s][:, v, :, :].rearrange("p t (c i) -> p c t i", i=4), in0=split4(f_pairs[s][:, v, :]),
                scalar1=om[:, k, pt : pt + 1], scalar2=None, op0=ALU.mult,
            )

        def squared(s, v):
            if v == 0:
                q_t[s] = qp.tile([128, 2, T, D // T], F32, name="q_pair")
            k = 2 * (s % PAIRS) + v
            pt = s // PAIRS
            nc.scalar.activation(
                q_t[s][:, v, :, :].rearrange("p t (c i) -> p c t i", i=4), split4(f_pairs[s][:, v, :]),
                ACT.Square, scale=rt[:, k, pt : pt + 1],
            )

        def sum_bank(pt, k, half):
            src = g_t if k < 2 else q_t
            g = k % 2
            if half == 0:
                bank[pt, k] = ps_a.tile([128, T, PT], F32, name="acc")
            acc = bank[pt, k]
            views = [v for v in range(V) if k >= 2 or v % 2 == 0 or v // 2 not in PRE_ADDED]
            for t in (2 * half, 2 * half + 1):
                for v in views:
                    nc.tensor.matmul(
                        acc[:, t, :], lhsT=src[PAIRS * pt + v // 2][:, v % 2, t, g * 128 : (g + 1) * 128], rhs=ident[:],
                        start=(v == views[0]), stop=(v == views[-1]), is_transpose=True,
                    )

        def stat_first(pt, k):
            acc = bank[pt, k]
            g = k % 2
            if k == 0:
                ab[pt] = sp.tile([128, 2, G, PT, T], BF16, name="ab", align_bytes=64)
            if k < 2:
                nc.vector.tensor_tensor(
                    out=ab[pt][:, 0, g, :, :], in0=acc[:].rearrange("d t p -> d p t"),
                    in1=gmv[:, g, :].unsqueeze(1).to_broadcast([128, PT, T]), op=ALU.mult,
                )
            else:
                var_t[pt, g] = sp.tile([128, T, PT], F32, name="var")
                nc.vector.tensor_tensor(out=var_t[pt, g][:], in0=acc[:], in1=musq[pt, g][:], op=ALU.subtract)

        def stat_second(pt, k):
            g = k % 2
            if k < 2:
                musq[pt, g] = sp.tile([128, T, PT], F32, name="musq")
                nc.scalar.activation(musq[pt, g][:], bank[pt, k][:], ACT.Square)
            else:
                nc.vector.tensor_tensor(
                    out=ab[pt][:, 1, g, :, :], in0=var_t[pt, g][:].rearrange("d t p -> d p t"),
                    in1=gvt[:, g, :].unsqueeze(1).to_broadcast([128, PT, T]), op=ALU.mult,
                )

        def quantize_ab(pt):
            cw = sp.tile([128, 2 * G * PT], U32, name="ab_codes", align_bytes=64)
            sc = sp.tile([128, 2 * G * PT], U8, name="ab_scales", align_bytes=64)
            nc.vector.quantize_mx(out=cw[:].bitcast(FP8X4), scales=sc[:], in_=ab[pt][:].rearrange("d x g p t -> d (x g p t)"))
            abc[pt] = (cw, sc)

        def product(acc, terms):
            n = len(terms) * G
            for j in range(n):
                lhs, nm, first = terms[j // G]
                g = j % G
                cols = slice((first + g) * 128, (first + g + 1) * 128)
                nc.tensor.matmul_mx(
                    out=acc[:], lhsT=lhs[0][:, cols].bitcast(FP8X4), lhsT_scale=lhs[1][:, cols],
                    rhs=codes_w[nm][:, g, :].bitcast(FP8X4), rhs_scale=scales_w[nm][:, g, :],
                    start=(j == 0), stop=(j == n - 1),
                )

        def c_product(pt):
            acc = ps_m.tile([128, H], F32, name="mm")
            product(acc, ((abc[pt], "wm", 0), (abc[pt], "wv", G)))
            c_ps[pt] = acc

        def c_copy(pt):
            c_sb[pt] = sp.tile([128, H], F32, name="c_sb")
            nc.scalar.copy(out=c_sb[pt][:], in_=c_ps[pt][:])

        def f_product(n, v):
            if n in WITH_C:
                acc = ps_a.tile([128, H], F32, name="acc")
                product(acc, ((codes[n], "wf", v * G), (abc[n // PAIRS], "wm", 0), (abc[n // PAIRS], "wv", G)))
            else:
                acc = ps_m.tile([128, H], F32, name="mm")
                product(acc, ((codes[n], "wf", v * G),))
            mm[n, v] = acc

        def add_c(n, v):
            if v == 0:
                e_t[n] = ep.tile([128, 2, H], F32, name="e", tag="e", align_bytes=64)
            nc.vector.tensor_tensor(out=e_t[n][:, v, :], in0=mm[n, v][:], in1=c_sb[n // PAIRS][:], op=ALU.add)

        def clamp(n):
            m_t[n] = ep.tile([128, 2, H], F32, name="m", tag="m", align_bytes=64)
            if n not in WITH_C and n not in BY_RELU:
                nc.vector.tensor_scalar(out=m_t[n][:], in0=e_t[n][:], scalar1=0.0, scalar2=None, op0=ALU.min)

        def exponential(n):
            if n in WITH_C:
                for v in range(2):
                    nc.scalar.activation(m_t[n][:, v, :], mm[n, v][:], ACT.Relu, scale=-1.0)
                nc.scalar.activation(m_t[n][:], m_t[n][:], ACT.Exp, scale=-1.0)
            elif n in BY_RELU:
                nc.scalar.activation(m_t[n][:], e_t[n][:], ACT.Relu, scale=-1.0)
                nc.scalar.activation(m_t[n][:], m_t[n][:], ACT.Exp, scale=-1.0)
            else:
                nc.scalar.activation(m_t[n][:], m_t[n][:], ACT.Exp)

        def finish(n):
            if n in WITH_C:
                for v in range(2):
                    nc.vector.scalar_tensor_tensor(
                        out=m_t[n][:, v, :], in0=m_t[n][:, v, :], scalar=-1.0, in1=mm[n, v][:], op0=ALU.add, op1=ALU.max
                    )
            else:
                nc.vector.scalar_tensor_tensor(out=m_t[n][:], in0=m_t[n][:], scalar=-1.0, in1=e_t[n][:], op0=ALU.add, op1=ALU.max)
            p0 = (n // PAIRS) * PT
            v0 = 2 * (n % PAIRS)
            nc.sync.dma_start(out=out[v0 : v0 + 2, p0 : p0 + PT, :].rearrange("v p h -> p v h"), in_=m_t[n][:])

        f_pairs[1] = load_pair(1)
        raws = {}
        grps = {}
        raws["wf", 0] = load_weight(wf, 0)
        f_pairs[2] = load_pair(2)
        raws["wf", 1] = load_weight(wf, 1)

        def load_late(i):
            if i < 2:
                raws["wm", i] = load_weight(wm, i)
            else:
                nc.sync.dma_start(out=wv8[:], in_=wv_bytes.rearrange("(g p t) n -> p g (t n)", p=128, t=T))

        def lay(i):
            key = (("wf", "wm", "wv")[i // 2], i % 2)
            if key[0] == "wv":
                raws[key] = widen_wv(key[1])
            grps[key] = interleave(raws[key])

        def quant_w(i):
            key = (("wf", "wm", "wv")[i // 2], i % 2)
            quantize_weight(grps[key], key[0], key[1])

        def adds(n, v):
            if n not in WITH_C:
                add_c(n, v)

        with tc.manual_schedule():
            for s in range(A_STEPS + 17):
                if 0 <= s - 4 < 3:
                    load_late(s - 4)
                if 0 <= s - 8 < A_STEPS:
                    evacuate(s - 8, 1)
                if 0 <= s - 16 < A_STEPS:
                    adds(s - 16, 0)
                if 0 <= s - 8 < 6:
                    quant_w(s - 8)
                if 0 <= s - 16 < A_STEPS:
                    adds(s - 16, 1)
                if 0 <= s - 9 < A_STEPS:
                    quantize_f(s - 9)
                if 0 <= s - 7 < 6:
                    lay(s - 7)
                if 0 <= s - 7 < A_STEPS:
                    evacuate(s - 7, 0)
                if 0 <= s - 15 < A_STEPS and (s - 15) % 4 == 0:
                    c_copy((s - 15) // 4)
                if 0 <= s - 16 < A_STEPS:
                    clamp(s - 16)
                if 0 <= s - 11 < 4 * NP:
                    stat_first((s - 11) // 4, (s - 11) % 4)
                if 0 <= s - 16 < A_STEPS:
                    exponential(s - 16)
                if 3 <= s - 4 < A_STEPS:
                    f_pairs[(s - 4)] = load_pair(s - 4)
                if 0 <= s - 15 < A_STEPS:
                    f_product(s - 15, 0)
                if 0 <= s - 7 < A_STEPS:
                    squared(s - 7, 0)
                if 0 <= s - 6 < A_STEPS:
                    weighted(s - 6, 0)
                if 0 <= s - 7 < A_STEPS:
                    transposes(s - 7, 1)
                if 0 <= s - 11 < 4 * NP:
                    stat_second((s - 11) // 4, (s - 11) % 4)
                if 0 <= s - 10 < 4 * NP:
                    sum_bank((s - 10) // 4, (s - 10) % 4, 0)
                if 0 <= s - 15 < A_STEPS:
                    f_product(s - 15, 1)
                if 0 <= s - 7 < A_STEPS:
                    squared(s - 7, 1)
                if 0 <= s - 6 < A_STEPS:
                    weighted(s - 6, 1)
                if 0 <= s - 14 < A_STEPS and (s - 14) % 4 == 0:
                    quantize_ab((s - 14) // 4)
                if 0 <= s - 6 < A_STEPS:
                    transposes(s - 6, 0)
                if 0 <= s - 17 < A_STEPS:
                    finish(s - 17)
                if 0 <= s - 10 < 4 * NP:
                    sum_bank((s - 10) // 4, (s - 10) % 4, 1)
                if 0 <= s - 14 < A_STEPS and (s - 14) % 4 == 0:
                    c_product((s - 14) // 4)
